import numpy as np
import ml_dtypes


def mxq(x, axis, fmt="e4m3"):
    dtype, down = {"e4m3": (ml_dtypes.float8_e4m3fn, 7), "e5m2": (ml_dtypes.float8_e5m2, 14)}[fmt]
    v = np.moveaxis(np.asarray(x, np.float32).astype(ml_dtypes.bfloat16).astype(np.float64), axis, -1)
    blocks = v.reshape(v.shape[:-1] + (-1, 32))
    amax = np.abs(blocks).max(-1, keepdims=True)
    byte = np.maximum(np.where(amax > 0, np.frexp(amax)[1] - 1 + 127, 0) - down, 1)
    scale = np.exp2(byte - 127.0)
    codes = (blocks / scale).astype(np.float32).astype(dtype).astype(np.float64)
    return np.moveaxis((codes * scale).reshape(v.shape), -1, axis)


WIDE = False


def mx_kscale(k):
    if not WIDE:
        return np.ones(k)
    levels = np.array([10, -10, 5, -5, 0])
    if k % 512:
        return np.exp2(np.random.permutation(np.resize(levels, k // 32))).repeat(32)
    a = np.empty((k // 512, 16))
    for p in range(k // 512):
        a[p, :8] = np.random.permutation(np.resize(levels, 8))
        for g in range(8):
            far = levels[np.abs(levels - a[p, g]) >= 10]
            a[p, g + 8] = far[np.random.randint(len(far))]
    return np.exp2(a.ravel()).repeat(32)


def f64(x):
    return np.asarray(x).astype(np.float64)


def striped(idx):
    return np.tile(np.asarray(idx).reshape(-1, 16).T, (8, 1)).astype(np.uint16)


def unstriped(offs):
    return offs[:16].T.reshape(-1).astype(np.int64)


E2M1 = np.array([0.0, 0.5, 1.0, 1.5, 2.0, 3.0, 4.0, 6.0, -0.0, -0.5, -1.0, -1.5, -2.0, -3.0, -4.0, -6.0])


def pack_weight(w, fmt):
    k, n = w.shape
    w = f64(np.asarray(w, np.float32).astype(ml_dtypes.bfloat16)).reshape(k // 32, 32, n)
    amax = np.abs(w).max(1)
    if fmt == "e4m3":
        byte = np.frexp(amax)[1] - 1 + 127 - 7
    else:
        mant, ex = np.frexp(amax / 6.0)
        byte = np.where(mant > 0.5, ex, ex - 1) + 127
    byte = np.clip(np.where(amax > 0, byte, 1), 1, 254)
    scaled = (w * np.exp2(127.0 - byte)[:, None, :]).reshape(k, n).astype(np.float32)
    by_word = np.ascontiguousarray(scaled.reshape(k // 512, 128, 4, n).transpose(0, 1, 3, 2))
    if fmt == "e4m3":
        words = by_word.astype(ml_dtypes.float8_e4m3fn).view(np.uint8)
    else:
        c = by_word.astype(ml_dtypes.float4_e2m1fn).view(np.uint8) & 0xF
        words = (c[..., 0::2] | (c[..., 1::2] << 4)).reshape(k // 512, 128, 2 * n)
    return np.ascontiguousarray(words), np.ascontiguousarray(byte.astype(np.uint8).reshape(k // 512, 16, n))


def unpack_weight(words, scales, fmt):
    g, _, n = scales.shape
    words = np.ascontiguousarray(words).reshape(g, 128, n, -1)
    if fmt == "e4m3":
        vals = words.view(ml_dtypes.float8_e4m3fn).astype(np.float64)
    else:
        nib = np.empty((g, 128, n, 4), np.uint8)
        nib[..., 0::2] = words & 0xF
        nib[..., 1::2] = words >> 4
        vals = E2M1[nib]
    vals = vals * np.repeat(np.exp2(scales.astype(np.float64) - 127.0), 8, axis=1)[..., None]
    return vals.transpose(0, 1, 3, 2).reshape(g * 512, n)


D, T, I, Q, M = 512, 2048, 512, 128, 2048


def setup_inputs():
    n = np.random.standard_normal
    idx = np.random.permutation(T)[:I]
    idx2 = np.random.permutation(T)[:I]
    idx3 = np.random.permutation(T)[:I]
    idx4 = np.random.permutation(M)[:I]
    fd = mx_kscale(D)
    keysp = pack_weight(n((D, T)) / fd[:, None], "e2m1")
    return {
        "query": (n((D, Q)) * 1.0 / np.sqrt(D) * fd[:, None]).astype(np.float32),
        "keys_words": keysp[0],
        "keys_scales": keysp[1],
        "lam": (np.random.uniform(0.3, 0.9, (Q, 1))).astype(np.float32),
        "pull": (np.random.uniform(0.3, 0.9, (Q, 1))).astype(np.float32),
        "old": (np.random.uniform(0.0, 2.0, (Q, M))).astype(np.float32),
        "fade": (np.random.uniform(0.3, 0.9, (Q, 1))).astype(np.float32),
        "offs": striped(idx),
        "offs2": striped(idx2),
        "offs3": striped(idx3),
        "offs4": striped(idx4),
    }


def reference(query, keys_words, keys_scales, lam, pull, old, fade, offs, offs2, offs3, offs4):
    idx = unstriped(offs)
    idx2 = unstriped(offs2)
    idx3 = unstriped(offs3)
    idx4 = unstriped(offs4)
    keysu = unpack_weight(keys_words, keys_scales, "e2m1")
    queryq = mxq(f64(query), 0, "e4m3")
    a = queryq.T @ keysu
    rv = np.log(np.exp(a[:, idx2]) + np.exp(a[:, idx3]))
    s = a[:, idx] - rv * f64(lam)
    p = np.exp(s - np.max(s, axis=1, keepdims=True))
    r = p / np.sum(p, axis=1, keepdims=True)
    r1 = np.pad(r, ((0, 0), (1, 0)))[:, :I]
    w = r - r1 * f64(pull)
    ws = w * 256.0
    wf = np.zeros((Q, M))
    wf[:, idx4] = ws
    y = f64(old) * f64(fade) + wf
    return y

@@ -1,0 +1,173 @@
+from contextlib import ExitStack
+
+import concourse.mybir as mybir
+
+D, T, I, Q, M = 512, 2048, 512, 128, 2048
+FLOPS = 2 * D * Q * T
+
+F32 = mybir.dt.float32
+BF16 = mybir.dt.bfloat16
+I32 = mybir.dt.int32
+U32 = mybir.dt.uint32
+U16 = mybir.dt.uint16
+U8 = mybir.dt.uint8
+FP8X4 = mybir.dt.float8_e4m3fn_x4
+FP4X4 = mybir.dt.float4_e2m1fn_x4
+ALU = mybir.AluOpType
+ACT = mybir.ActivationFunctionType
+
+P = 128
+PACK = 4
+PER_COL = 16
+PASS_WIDTHS = (512, 512, 512, 256, 128, 128)
+WORD_HALF = T // 2
+GATHER_CUTS = (0, 256, 512)
+SCATTER_CUTS = (0, 160, 512)
+STORE_CUTS = (0, 256, 768, 1280, 1792, 2048)
+
+
+def spans(cuts):
+    return list(zip(cuts[:-1], cuts[1:]))
+
+
+def tile_attend_tworivals_stepwise_counts_kernel(
+    tc, query, keys_words, keys_scales, lam, pull, old, fade, offs, offs2, offs3, offs4, out
+):
+    nc = tc.nc
+    with ExitStack() as ctx:
+        pool = ctx.enter_context(tc.tile_pool(name="held", bufs=1))
+        psum = ctx.enter_context(tc.psum_pool(name="psum", bufs=1))
+
+        key_scales = pool.tile([P, T], U8, name="key_scales", align_bytes=64)
+        nc.vector.memset(key_scales[:].bitcast(I32), 0)
+
+        query_raw = pool.tile([P, PACK, Q], F32, name="query_raw")
+        nc.sync.dma_start(out=query_raw[:], in_=query.rearrange("(p j) q -> p j q", j=PACK))
+        for quad in range(4):
+            nc.scalar.dma_start(
+                out=key_scales[32 * quad : 32 * quad + 4, :].bitcast(I32),
+                in_=keys_scales[0, 4 * quad : 4 * quad + 4, :].bitcast(I32),
+            )
+        key_words = []
+        for half in range(2):
+            words = pool.tile([P, 2 * WORD_HALF], U8, name="key_words%d" % half, align_bytes=64)
+            nc.sync.dma_start(
+                out=words[:].bitcast(I32),
+                in_=keys_words[0, :, 2 * WORD_HALF * half : 2 * WORD_HALF * (half + 1)].bitcast(I32),
+            )
+            key_words.append(words)
+
+        list2 = pool.tile([P, I // PER_COL], U16, name="list2")
+        nc.sync.dma_start(list2[:], offs2)
+        list3 = pool.tile([P, I // PER_COL], U16, name="list3")
+        nc.sync.dma_start(list3[:], offs3)
+        list1 = pool.tile([P, I // PER_COL], U16, name="list1")
+        nc.sync.dma_start(list1[:], offs)
+        lam_col = pool.tile([P, 1], F32, name="lam_col")
+        nc.sync.dma_start(lam_col[:], lam)
+        pull_col = pool.tile([P, 1], F32, name="pull_col")
+        nc.sync.dma_start(pull_col[:], pull)
+        list4 = pool.tile([P, I // PER_COL], U16, name="list4")
+        nc.sync.dma_start(list4[:], offs4)
+        fade_col = pool.tile([P, 1], F32, name="fade_col")
+        nc.sync.dma_start(fade_col[:], fade)
+        old_sb = pool.tile([P, M], F32, name="old_sb")
+        nc.sync.dma_start(old_sb[:], old)
+
+        placed = pool.tile([P, M], F32, name="placed")
+        nc.vector.memset(placed[:], 0.0)
+        pulled = pool.tile([P, I], F32, name="pulled")
+        nc.vector.memset(pulled[:, 0:1], 0.0)
+
+        grouped = pool.tile([P, Q, PACK], BF16, name="grouped", align_bytes=64)
+        nc.vector.tensor_copy(
+            out=grouped[:].rearrange("p (c i) t -> p c t i", i=4),
+            in_=query_raw[:].rearrange("p t (c i) -> p c t i", i=4),
+        )
+        query_codes = pool.tile([P, Q], U32, name="query_codes", align_bytes=64)
+        query_scales = pool.tile([P, Q], U8, name="query_scales", align_bytes=64)
+        nc.vector.quantize_mx(
+            out=query_codes[:].bitcast(FP8X4),
+            scales=query_scales[:],
+            in_=grouped[:].rearrange("p q t -> p (q t)"),
+        )
+
+        scores = pool.tile([P, T], F32, name="scores")
+        start = 0
+        for n, width in enumerate(PASS_WIDTHS):
+            bank = psum.tile([P, width], F32, name="bank%d" % n)
+            half, first = divmod(start, WORD_HALF)
+            nc.tensor.matmul_mx(
+                out=bank[:],
+                lhsT=query_codes[:].bitcast(FP8X4),
+                lhsT_scale=query_scales[:],
+                rhs=key_words[half][:, 2 * first : 2 * (first + width)].bitcast(FP4X4),
+                rhs_scale=key_scales[:, start : start + width],
+                start=True,
+                stop=True,
+            )
+            if n % 2 == 0:
+                nc.scalar.copy(out=scores[:, start : start + width], in_=bank[:])
+            else:
+                nc.vector.tensor_copy(out=scores[:, start : start + width], in_=bank[:])
+            start = start + width
+
+        def listed(window, offsets, lo, hi):
+            return window[:].indirect(offsets[:, lo // PER_COL : hi // PER_COL])
+
+        neg_pull = pool.tile([P, 1], F32, name="neg_pull")
+        nc.vector.tensor_scalar(neg_pull[:], pull_col[:], -1.0, None, ALU.mult)
+
+        rival2 = pool.tile([P, I], F32, name="rival2", tag="gathered")
+        gap = pool.tile([P, I], F32, name="gap")
+        tanh_gap = pool.tile([P, I], F32, name="tanh_gap")
+        for lo, hi in spans(GATHER_CUTS):
+            nc.vector.tensor_copy(rival2[:, lo:hi], listed(scores, list2, lo, hi))
+        for lo, hi in spans(GATHER_CUTS):
+            nc.vector.tensor_tensor(gap[:, lo:hi], listed(scores, list3, lo, hi), rival2[:, lo:hi], ALU.subtract)
+            nc.scalar.activation(tanh_gap[:, lo:hi], gap[:, lo:hi], ACT.Tanh, scale=0.5)
+
+        larger = pool.tile([P, I], F32, name="larger")
+        nc.vector.scalar_tensor_tensor(larger[:], gap[:], 0.0, rival2[:], ALU.max, ALU.add)
+        abs_tanh = pool.tile([P, I], F32, name="abs_tanh")
+        nc.vector.scalar_tensor_tensor(abs_tanh[:], tanh_gap[:], -1.0, tanh_gap[:], ALU.mult, ALU.max)
+        log_share = pool.tile([P, I], F32, name="log_share")
+        nc.scalar.activation(log_share[:], abs_tanh[:], ACT.Ln, bias=0.5, scale=0.5)
+
+        own = pool.tile([P, I], F32, name="own", tag="gathered")
+        nc.vector.tensor_copy(own[:], listed(scores, list1, 0, I))
+        neg_partial = pool.tile([P, I], F32, name="neg_partial")
+        nc.vector.scalar_tensor_tensor(neg_partial[:], larger[:], lam_col[:], own[:], ALU.mult, ALU.subtract)
+        slot_scores = pool.tile([P, I], F32, name="slot_scores", tag="late")
+        nc.vector.scalar_tensor_tensor(
+            slot_scores[:], log_share[:], lam_col[:], neg_partial[:], ALU.mult, ALU.subtract
+        )
+        neg_max = pool.tile([P, 1], F32, name="neg_max")
+        nc.vector.tensor_reduce(neg_max[:], slot_scores[:], mybir.AxisListType.X, ALU.max, negate=True)
+
+        shares = pool.tile([P, I], F32, name="shares")
+        sums = pool.tile([P, 2], F32, name="sums")
+        for n, (lo, hi) in enumerate(spans(SCATTER_CUTS)):
+            nc.scalar.activation(
+                shares[:, lo:hi], slot_scores[:, lo:hi], ACT.Exp, bias=neg_max[:], accum_out=sums[:, n : n + 1]
+            )
+            last = min(hi, I - 1)
+            nc.scalar.activation(pulled[:, lo + 1 : last + 1], shares[:, lo:last], ACT.Copy, scale=neg_pull[:])
+            nc.vector.tensor_tensor(listed(placed, list4, lo, hi), shares[:, lo:hi], pulled[:, lo:hi], ALU.add)
+
+        total = pool.tile([P, 1], F32, name="total")
+        nc.scalar.activation(total[:], sums[:, 0:1], ACT.Identity, bias=sums[:, 1:2])
+        total_256 = pool.tile([P, 1], F32, name="total_256")
+        nc.scalar.activation(total_256[:], total[:], ACT.Copy, scale=1.0 / 256.0)
+        norm = pool.tile([P, 1], F32, name="norm")
+        nc.vector.reciprocal(norm[:], total_256[:])
+
+        faded = pool.tile([P, M], F32, name="faded", tag="late")
+        result = pool.tile([P, M], F32, name="result")
+        for lo, hi in spans(STORE_CUTS):
+            nc.scalar.activation(faded[:, lo:hi], old_sb[:, lo:hi], ACT.Copy, scale=fade_col[:])
+        for lo, hi in spans(STORE_CUTS):
+            nc.vector.scalar_tensor_tensor(
+                result[:, lo:hi], placed[:, lo:hi], norm[:], faded[:, lo:hi], ALU.mult, ALU.add
+            )
+            nc.sync.dma_start(out=out[:, lo:hi], in_=result[:, lo:hi])

@@ -22,8 +22,10 @@ PER_COL = 16
 PASS_WIDTHS = (512, 512, 512, 256, 128, 128)
 WORD_HALF = T // 2
 GATHER_CUTS = (0, 256, 512)
-SCATTER_CUTS = (0, 160, 512)
-STORE_CUTS = (0, 256, 768, 1280, 1792, 2048)
+GAP_CUTS = (0, 256, 448, 512)
+EXP_CUTS = (0, 128, 256, 512)
+SCATTER_CUTS = (0, 128, 512)
+STORE_CUTS = (0, 128, 512, 1024, 1536, 1920, 2048)
 
 
 def spans(cuts):
@@ -44,7 +46,7 @@ def tile_attend_tworivals_stepwise_counts_kernel(
         query_raw = pool.tile([P, PACK, Q], F32, name="query_raw")
         nc.sync.dma_start(out=query_raw[:], in_=query.rearrange("(p j) q -> p j q", j=PACK))
         for quad in range(4):
-            nc.scalar.dma_start(
+            nc.sync.dma_start(
                 out=key_scales[32 * quad : 32 * quad + 4, :].bitcast(I32),
                 in_=keys_scales[0, 4 * quad : 4 * quad + 4, :].bitcast(I32),
             )
@@ -118,47 +120,57 @@ def tile_attend_tworivals_stepwise_counts_kernel(
         neg_pull = pool.tile([P, 1], F32, name="neg_pull")
         nc.vector.tensor_scalar(neg_pull[:], pull_col[:], -1.0, None, ALU.mult)
 
+        sums = pool.tile([P, 3], F32, name="sums")
+        nc.vector.tensor_scalar(sums[:, 2:3], pull_col[:], -1.0, None, ALU.mult)
+
         rival2 = pool.tile([P, I], F32, name="rival2", tag="gathered")
         gap = pool.tile([P, I], F32, name="gap")
         tanh_gap = pool.tile([P, I], F32, name="tanh_gap")
         for lo, hi in spans(GATHER_CUTS):
             nc.vector.tensor_copy(rival2[:, lo:hi], listed(scores, list2, lo, hi))
-        for lo, hi in spans(GATHER_CUTS):
+        for lo, hi in spans(GAP_CUTS):
             nc.vector.tensor_tensor(gap[:, lo:hi], listed(scores, list3, lo, hi), rival2[:, lo:hi], ALU.subtract)
             nc.scalar.activation(tanh_gap[:, lo:hi], gap[:, lo:hi], ACT.Tanh, scale=0.5)
 
         larger = pool.tile([P, I], F32, name="larger")
-        nc.vector.scalar_tensor_tensor(larger[:], gap[:], 0.0, rival2[:], ALU.max, ALU.add)
+        for lo, hi in spans(GATHER_CUTS):
+            nc.vector.scalar_tensor_tensor(larger[:, lo:hi], gap[:, lo:hi], 0.0, rival2[:, lo:hi], ALU.max, ALU.add)
         abs_tanh = pool.tile([P, I], F32, name="abs_tanh")
         nc.vector.scalar_tensor_tensor(abs_tanh[:], tanh_gap[:], -1.0, tanh_gap[:], ALU.mult, ALU.max)
         log_share = pool.tile([P, I], F32, name="log_share")
         nc.scalar.activation(log_share[:], abs_tanh[:], ACT.Ln, bias=0.5, scale=0.5)
 
         own = pool.tile([P, I], F32, name="own", tag="gathered")
-        nc.vector.tensor_copy(own[:], listed(scores, list1, 0, I))
+        for lo, hi in spans(GATHER_CUTS):
+            nc.vector.tensor_copy(own[:, lo:hi], listed(scores, list1, lo, hi))
         neg_partial = pool.tile([P, I], F32, name="neg_partial")
-        nc.vector.scalar_tensor_tensor(neg_partial[:], larger[:], lam_col[:], own[:], ALU.mult, ALU.subtract)
+        for lo, hi in spans(GATHER_CUTS):
+            nc.vector.scalar_tensor_tensor(
+                neg_partial[:, lo:hi], larger[:, lo:hi], lam_col[:], own[:, lo:hi], ALU.mult, ALU.subtract
+            )
         slot_scores = pool.tile([P, I], F32, name="slot_scores", tag="late")
-        nc.vector.scalar_tensor_tensor(
-            slot_scores[:], log_share[:], lam_col[:], neg_partial[:], ALU.mult, ALU.subtract
-        )
+        for lo, hi in spans(GATHER_CUTS):
+            nc.vector.scalar_tensor_tensor(
+                slot_scores[:, lo:hi], log_share[:, lo:hi], lam_col[:], neg_partial[:, lo:hi], ALU.mult, ALU.subtract
+            )
         neg_max = pool.tile([P, 1], F32, name="neg_max")
         nc.vector.tensor_reduce(neg_max[:], slot_scores[:], mybir.AxisListType.X, ALU.max, negate=True)
 
         shares = pool.tile([P, I], F32, name="shares")
-        sums = pool.tile([P, 2], F32, name="sums")
-        for n, (lo, hi) in enumerate(spans(SCATTER_CUTS)):
+        scatter_starts = {hi: lo for lo, hi in spans(SCATTER_CUTS)}
+        for n, (first, hi) in enumerate(spans(EXP_CUTS)):
             nc.scalar.activation(
-                shares[:, lo:hi], slot_scores[:, lo:hi], ACT.Exp, bias=neg_max[:], accum_out=sums[:, n : n + 1]
+                shares[:, first:hi], slot_scores[:, first:hi], ACT.Exp, bias=neg_max[:], accum_out=sums[:, n : n + 1]
             )
-            last = min(hi, I - 1)
-            nc.scalar.activation(pulled[:, lo + 1 : last + 1], shares[:, lo:last], ACT.Copy, scale=neg_pull[:])
-            nc.vector.tensor_tensor(listed(placed, list4, lo, hi), shares[:, lo:hi], pulled[:, lo:hi], ALU.add)
+            if hi in scatter_starts:
+                lo = scatter_starts[hi]
+                last = min(hi, I - 1)
+                nc.scalar.activation(pulled[:, lo + 1 : last + 1], shares[:, lo:last], ACT.Copy, scale=sums[:, 2:3] if lo == 0 else neg_pull[:])
+                nc.vector.tensor_tensor(listed(placed, list4, lo, hi), shares[:, lo:hi], pulled[:, lo:hi], ALU.add)
 
-        total = pool.tile([P, 1], F32, name="total")
-        nc.scalar.activation(total[:], sums[:, 0:1], ACT.Identity, bias=sums[:, 1:2])
+        sums_256 = pool.tile([P, 3], F32, name="sums_256")
         total_256 = pool.tile([P, 1], F32, name="total_256")
-        nc.scalar.activation(total_256[:], total[:], ACT.Copy, scale=1.0 / 256.0)
+        nc.scalar.activation(sums_256[:], sums[:], ACT.Copy, scale=1.0 / 256.0, accum_out=total_256[:])
         norm = pool.tile([P, 1], F32, name="norm")
         nc.vector.reciprocal(norm[:], total_256[:])
 

from contextlib import ExitStack

import concourse.mybir as mybir

D, T, I, Q, M = 512, 2048, 512, 128, 2048
FLOPS = 2 * D * Q * T

F32 = mybir.dt.float32
BF16 = mybir.dt.bfloat16
I32 = mybir.dt.int32
U32 = mybir.dt.uint32
U16 = mybir.dt.uint16
U8 = mybir.dt.uint8
FP8X4 = mybir.dt.float8_e4m3fn_x4
FP4X4 = mybir.dt.float4_e2m1fn_x4
ALU = mybir.AluOpType
ACT = mybir.ActivationFunctionType

P = 128
PACK = 4
PER_COL = 16
PASS_WIDTHS = (512, 512, 512, 256, 128, 128)
WORD_HALF = T // 2
GATHER_CUTS = (0, 256, 512)
GAP_CUTS = (0, 256, 448, 512)
EXP_CUTS = (0, 128, 256, 512)
SCATTER_CUTS = (0, 128, 512)
STORE_CUTS = (0, 128, 512, 1024, 1536, 1920, 2048)


def spans(cuts):
    return list(zip(cuts[:-1], cuts[1:]))


def tile_attend_tworivals_stepwise_counts_kernel(
    tc, query, keys_words, keys_scales, lam, pull, old, fade, offs, offs2, offs3, offs4, out
):
    nc = tc.nc
    with ExitStack() as ctx:
        pool = ctx.enter_context(tc.tile_pool(name="held", bufs=1))
        psum = ctx.enter_context(tc.psum_pool(name="psum", bufs=1))

        key_scales = pool.tile([P, T], U8, name="key_scales", align_bytes=64)
        nc.vector.memset(key_scales[:].bitcast(I32), 0)

        query_raw = pool.tile([P, PACK, Q], F32, name="query_raw")
        nc.sync.dma_start(out=query_raw[:], in_=query.rearrange("(p j) q -> p j q", j=PACK))
        for quad in range(4):
            nc.sync.dma_start(
                out=key_scales[32 * quad : 32 * quad + 4, :].bitcast(I32),
                in_=keys_scales[0, 4 * quad : 4 * quad + 4, :].bitcast(I32),
            )
        key_words = []
        for half in range(2):
            words = pool.tile([P, 2 * WORD_HALF], U8, name="key_words%d" % half, align_bytes=64)
            nc.sync.dma_start(
                out=words[:].bitcast(I32),
                in_=keys_words[0, :, 2 * WORD_HALF * half : 2 * WORD_HALF * (half + 1)].bitcast(I32),
            )
            key_words.append(words)

        list2 = pool.tile([P, I // PER_COL], U16, name="list2")
        nc.sync.dma_start(list2[:], offs2)
        list3 = pool.tile([P, I // PER_COL], U16, name="list3")
        nc.sync.dma_start(list3[:], offs3)
        list1 = pool.tile([P, I // PER_COL], U16, name="list1")
        nc.sync.dma_start(list1[:], offs)
        lam_col = pool.tile([P, 1], F32, name="lam_col")
        nc.sync.dma_start(lam_col[:], lam)
        pull_col = pool.tile([P, 1], F32, name="pull_col")
        nc.sync.dma_start(pull_col[:], pull)
        list4 = pool.tile([P, I // PER_COL], U16, name="list4")
        nc.sync.dma_start(list4[:], offs4)
        fade_col = pool.tile([P, 1], F32, name="fade_col")
        nc.sync.dma_start(fade_col[:], fade)
        old_sb = pool.tile([P, M], F32, name="old_sb")
        nc.sync.dma_start(old_sb[:], old)

        placed = pool.tile([P, M], F32, name="placed")
        nc.vector.memset(placed[:], 0.0)
        pulled = pool.tile([P, I], F32, name="pulled")
        nc.vector.memset(pulled[:, 0:1], 0.0)

        grouped = pool.tile([P, Q, PACK], BF16, name="grouped", align_bytes=64)
        nc.vector.tensor_copy(
            out=grouped[:].rearrange("p (c i) t -> p c t i", i=4),
            in_=query_raw[:].rearrange("p t (c i) -> p c t i", i=4),
        )
        query_codes = pool.tile([P, Q], U32, name="query_codes", align_bytes=64)
        query_scales = pool.tile([P, Q], U8, name="query_scales", align_bytes=64)
        nc.vector.quantize_mx(
            out=query_codes[:].bitcast(FP8X4),
            scales=query_scales[:],
            in_=grouped[:].rearrange("p q t -> p (q t)"),
        )

        scores = pool.tile([P, T], F32, name="scores")
        start = 0
        for n, width in enumerate(PASS_WIDTHS):
            bank = psum.tile([P, width], F32, name="bank%d" % n)
            half, first = divmod(start, WORD_HALF)
            nc.tensor.matmul_mx(
                out=bank[:],
                lhsT=query_codes[:].bitcast(FP8X4),
                lhsT_scale=query_scales[:],
                rhs=key_words[half][:, 2 * first : 2 * (first + width)].bitcast(FP4X4),
                rhs_scale=key_scales[:, start : start + width],
                start=True,
                stop=True,
            )
            if n % 2 == 0:
                nc.scalar.copy(out=scores[:, start : start + width], in_=bank[:])
            else:
                nc.vector.tensor_copy(out=scores[:, start : start + width], in_=bank[:])
            start = start + width

        def listed(window, offsets, lo, hi):
            return window[:].indirect(offsets[:, lo // PER_COL : hi // PER_COL])

        neg_pull = pool.tile([P, 1], F32, name="neg_pull")
        nc.vector.tensor_scalar(neg_pull[:], pull_col[:], -1.0, None, ALU.mult)

        sums = pool.tile([P, 3], F32, name="sums")
        nc.vector.tensor_scalar(sums[:, 2:3], pull_col[:], -1.0, None, ALU.mult)

        rival2 = pool.tile([P, I], F32, name="rival2", tag="gathered")
        gap = pool.tile([P, I], F32, name="gap")
        tanh_gap = pool.tile([P, I], F32, name="tanh_gap")
        for lo, hi in spans(GATHER_CUTS):
            nc.vector.tensor_copy(rival2[:, lo:hi], listed(scores, list2, lo, hi))
        for lo, hi in spans(GAP_CUTS):
            nc.vector.tensor_tensor(gap[:, lo:hi], listed(scores, list3, lo, hi), rival2[:, lo:hi], ALU.subtract)
            nc.scalar.activation(tanh_gap[:, lo:hi], gap[:, lo:hi], ACT.Tanh, scale=0.5)

        larger = pool.tile([P, I], F32, name="larger")
        for lo, hi in spans(GATHER_CUTS):
            nc.vector.scalar_tensor_tensor(larger[:, lo:hi], gap[:, lo:hi], 0.0, rival2[:, lo:hi], ALU.max, ALU.add)
        abs_tanh = pool.tile([P, I], F32, name="abs_tanh")
        nc.vector.scalar_tensor_tensor(abs_tanh[:], tanh_gap[:], -1.0, tanh_gap[:], ALU.mult, ALU.max)
        log_share = pool.tile([P, I], F32, name="log_share")
        nc.scalar.activation(log_share[:], abs_tanh[:], ACT.Ln, bias=0.5, scale=0.5)

        own = pool.tile([P, I], F32, name="own", tag="gathered")
        for lo, hi in spans(GATHER_CUTS):
            nc.vector.tensor_copy(own[:, lo:hi], listed(scores, list1, lo, hi))
        neg_partial = pool.tile([P, I], F32, name="neg_partial")
        for lo, hi in spans(GATHER_CUTS):
            nc.vector.scalar_tensor_tensor(
                neg_partial[:, lo:hi], larger[:, lo:hi], lam_col[:], own[:, lo:hi], ALU.mult, ALU.subtract
            )
        slot_scores = pool.tile([P, I], F32, name="slot_scores", tag="late")
        for lo, hi in spans(GATHER_CUTS):
            nc.vector.scalar_tensor_tensor(
                slot_scores[:, lo:hi], log_share[:, lo:hi], lam_col[:], neg_partial[:, lo:hi], ALU.mult, ALU.subtract
            )
        neg_max = pool.tile([P, 1], F32, name="neg_max")
        nc.vector.tensor_reduce(neg_max[:], slot_scores[:], mybir.AxisListType.X, ALU.max, negate=True)

        shares = pool.tile([P, I], F32, name="shares")
        scatter_starts = {hi: lo for lo, hi in spans(SCATTER_CUTS)}
        for n, (first, hi) in enumerate(spans(EXP_CUTS)):
            nc.scalar.activation(
                shares[:, first:hi], slot_scores[:, first:hi], ACT.Exp, bias=neg_max[:], accum_out=sums[:, n : n + 1]
            )
            if hi in scatter_starts:
                lo = scatter_starts[hi]
                last = min(hi, I - 1)
                nc.scalar.activation(pulled[:, lo + 1 : last + 1], shares[:, lo:last], ACT.Copy, scale=sums[:, 2:3] if lo == 0 else neg_pull[:])
                nc.vector.tensor_tensor(listed(placed, list4, lo, hi), shares[:, lo:hi], pulled[:, lo:hi], ALU.add)

        sums_256 = pool.tile([P, 3], F32, name="sums_256")
        total_256 = pool.tile([P, 1], F32, name="total_256")
        nc.scalar.activation(sums_256[:], sums[:], ACT.Copy, scale=1.0 / 256.0, accum_out=total_256[:])
        norm = pool.tile([P, 1], F32, name="norm")
        nc.vector.reciprocal(norm[:], total_256[:])

        faded = pool.tile([P, M], F32, name="faded", tag="late")
        result = pool.tile([P, M], F32, name="result")
        for lo, hi in spans(STORE_CUTS):
            nc.scalar.activation(faded[:, lo:hi], old_sb[:, lo:hi], ACT.Copy, scale=fade_col[:])
        for lo, hi in spans(STORE_CUTS):
            nc.vector.scalar_tensor_tensor(
                result[:, lo:hi], placed[:, lo:hi], norm[:], faded[:, lo:hi], ALU.mult, ALU.add
            )
            nc.sync.dma_start(out=out[:, lo:hi], in_=result[:, lo:hi])
